import numpy as np
import ml_dtypes


def mxq(x, axis, fmt="e4m3"):
    dtype, down = {"e4m3": (ml_dtypes.float8_e4m3fn, 7), "e5m2": (ml_dtypes.float8_e5m2, 14)}[fmt]
    v = np.moveaxis(np.asarray(x, np.float32).astype(ml_dtypes.bfloat16).astype(np.float64), axis, -1)
    blocks = v.reshape(v.shape[:-1] + (-1, 32))
    amax = np.abs(blocks).max(-1, keepdims=True)
    byte = np.maximum(np.where(amax > 0, np.frexp(amax)[1] - 1 + 127, 0) - down, 1)
    scale = np.exp2(byte - 127.0)
    codes = (blocks / scale).astype(np.float32).astype(dtype).astype(np.float64)
    return np.moveaxis((codes * scale).reshape(v.shape), -1, axis)


WIDE = False


def mx_kscale(k):
    if not WIDE:
        return np.ones(k)
    levels = np.array([10, -10, 5, -5, 0])
    if k % 512:
        return np.exp2(np.random.permutation(np.resize(levels, k // 32))).repeat(32)
    a = np.empty((k // 512, 16))
    for p in range(k // 512):
        a[p, :8] = np.random.permutation(np.resize(levels, 8))
        for g in range(8):
            far = levels[np.abs(levels - a[p, g]) >= 10]
            a[p, g + 8] = far[np.random.randint(len(far))]
    return np.exp2(a.ravel()).repeat(32)


def f64(x):
    return np.asarray(x).astype(np.float64)


def striped(idx):
    return np.tile(np.asarray(idx).reshape(-1, 16).T, (8, 1)).astype(np.uint16)


def unstriped(offs):
    return offs[:16].T.reshape(-1).astype(np.int64)


E2M1 = np.array([0.0, 0.5, 1.0, 1.5, 2.0, 3.0, 4.0, 6.0, -0.0, -0.5, -1.0, -1.5, -2.0, -3.0, -4.0, -6.0])


def pack_weight(w, fmt):
    k, n = w.shape
    w = f64(np.asarray(w, np.float32).astype(ml_dtypes.bfloat16)).reshape(k // 32, 32, n)
    amax = np.abs(w).max(1)
    if fmt == "e4m3":
        byte = np.frexp(amax)[1] - 1 + 127 - 7
    else:
        mant, ex = np.frexp(amax / 6.0)
        byte = np.where(mant > 0.5, ex, ex - 1) + 127
    byte = np.clip(np.where(amax > 0, byte, 1), 1, 254)
    scaled = (w * np.exp2(127.0 - byte)[:, None, :]).reshape(k, n).astype(np.float32)
    by_word = np.ascontiguousarray(scaled.reshape(k // 512, 128, 4, n).transpose(0, 1, 3, 2))
    if fmt == "e4m3":
        words = by_word.astype(ml_dtypes.float8_e4m3fn).view(np.uint8)
    else:
        c = by_word.astype(ml_dtypes.float4_e2m1fn).view(np.uint8) & 0xF
        words = (c[..., 0::2] | (c[..., 1::2] << 4)).reshape(k // 512, 128, 2 * n)
    return np.ascontiguousarray(words), np.ascontiguousarray(byte.astype(np.uint8).reshape(k // 512, 16, n))


def unpack_weight(words, scales, fmt):
    g, _, n = scales.shape
    words = np.ascontiguousarray(words).reshape(g, 128, n, -1)
    if fmt == "e4m3":
        vals = words.view(ml_dtypes.float8_e4m3fn).astype(np.float64)
    else:
        nib = np.empty((g, 128, n, 4), np.uint8)
        nib[..., 0::2] = words & 0xF
        nib[..., 1::2] = words >> 4
        vals = E2M1[nib]
    vals = vals * np.repeat(np.exp2(scales.astype(np.float64) - 127.0), 8, axis=1)[..., None]
    return vals.transpose(0, 1, 3, 2).reshape(g * 512, n)


D, E, T, I, Q, G = 512, 512, 2048, 512, 128, 32


def setup_inputs():
    n = np.random.standard_normal
    idx = np.random.permutation(T)[:I]
    fd = mx_kscale(D)
    fe = mx_kscale(E)
    keysp = pack_weight(n((D, T)) / fd[:, None], "e4m3")
    valsp = pack_weight(n((E, T)) / fe[:, None], "e4m3")
    return {
        "query": (n((D, Q)) * 0.6 / np.sqrt(D) * fd[:, None]).astype(np.float32),
        "keys_words": keysp[0],
        "keys_scales": keysp[1],
        "trust": (np.random.uniform(0.3, 1.0, (Q, 1))).astype(np.float32),
        "gout": (n((E, Q)) * 1 / np.sqrt(E) * fe[:, None]).astype(np.float32),
        "vals_words": valsp[0],
        "vals_scales": valsp[1],
        "size": (np.random.uniform(0.5, 2.0, (1, I))).astype(np.float32),
        "old": (0.5 * n((Q, T))).astype(np.float32),
        "offs": striped(idx),
    }


def reference(query, keys_words, keys_scales, trust, gout, vals_words, vals_scales, size, old, offs):
    idx = unstriped(offs)
    keysu = unpack_weight(keys_words, keys_scales, "e4m3")
    valsu = unpack_weight(vals_words, vals_scales, "e4m3")
    queryq = mxq(f64(query), 0, "e4m3")
    keysidxg = keysu[:, idx]
    a = queryq.T @ keysidxg
    s = a.reshape(Q, G, I // G).mean(axis=2) * f64(trust)
    sr = np.repeat(s, I // G, axis=1)
    b = a - sr
    p = np.exp(b - np.max(b, axis=1, keepdims=True))
    z = np.sum(p, axis=1, keepdims=True)
    goutq = mxq(f64(gout), 0, "e4m3")
    valsidxg = valsu[:, idx]
    c0 = goutq.T @ valsidxg
    dz = np.sum(c0 * p * f64(size) / np.square(z) * (-1.0), axis=1, keepdims=True)
    dp = c0 / z * f64(size) + dz
    db = dp * p
    dsr = db * (-1.0)
    ds = dsr.reshape(Q, G, I // G).sum(axis=2)
    e1 = ds * f64(trust) / 16.0
    r1 = np.repeat(e1, I // G, axis=1)
    da = db + r1
    gs = da * 512.0
    gf = np.zeros((Q, T))
    gf[:, idx] = gs
    y = f64(old) + gf
    return y

@@ -1,0 +1,158 @@
+from contextlib import ExitStack
+
+import concourse.mybir as mybir
+from concourse.masks import make_identity
+
+D, T, I, Q, G = 512, 2048, 512, 128, 32
+FLOPS = 2 * 2 * D * I * Q
+
+F32 = mybir.dt.float32
+BF16 = mybir.dt.bfloat16
+I32 = mybir.dt.int32
+U32 = mybir.dt.uint32
+U16 = mybir.dt.uint16
+U8 = mybir.dt.uint8
+FP8X4 = mybir.dt.float8_e4m3fn_x4
+ALU = mybir.AluOpType
+ACT = mybir.ActivationFunctionType
+AX = mybir.AxisListType
+
+P = 128
+PACK = 4
+PAGE = I // G
+HALF = I // 2
+HG = G // 2
+VAL_ROW = 4
+OUT_CHUNKS = [256, 512, 640, 640]
+
+
+def tile_attend_bpagecentred_s_kernel(tc, query, keys_words, keys_scales, trust, gout, vals_words, vals_scales, size, old, offs, out):
+    nc = tc.nc
+    with ExitStack() as ctx:
+        sb = ctx.enter_context(tc.tile_pool(name="sb", bufs=1))
+        ps = ctx.enter_context(tc.psum_pool(name="ps", bufs=1))
+
+        offsets = sb.tile([P, I // 16], U16, name="offsets")
+        nc.sync.dma_start(offsets[:], offs)
+
+        ks = sb.tile([P, T], U8, name="ks", align_bytes=64)
+        vs = sb.tile([P, T], U8, name="vs", align_bytes=64)
+        gf = sb.tile([P, T], F32, name="gf", align_bytes=64)
+        nc.vector.memset(ks[:].bitcast(I32), 0)
+        nc.vector.memset(vs[:].bitcast(I32), 0)
+        nc.vector.memset(gf[:], 0.0)
+
+        for r in range(4):
+            nc.scalar.dma_start(ks[32 * r : 32 * r + 4, :].bitcast(I32), keys_scales[0, 4 * r : 4 * r + 4, :].bitcast(I32))
+
+        q_raw = sb.tile([P, PACK, Q], F32, name="q_raw")
+        nc.sync.dma_start(q_raw[:], query.rearrange("(p j) w -> p j w", j=PACK))
+        kw = sb.tile([P, T], I32, name="kw", align_bytes=64)
+        nc.sync.dma_start(kw[:], keys_words[0].rearrange("p n t -> p (n t)").bitcast(I32))
+        for r in range(4):
+            nc.sync.dma_start(vs[32 * r + VAL_ROW : 32 * r + VAL_ROW + 4, :].bitcast(I32), vals_scales[0, 4 * r : 4 * r + 4, :].bitcast(I32))
+        g_raw = sb.tile([P, PACK, Q], F32, name="g_raw")
+        nc.sync.dma_start(g_raw[:], gout.rearrange("(p j) w -> p j w", j=PACK))
+        vw = sb.tile([P, T], I32, name="vw", align_bytes=64)
+        nc.sync.dma_start(vw[:], vals_words[0].rearrange("p n t -> p (n t)").bitcast(I32))
+        old_sb = sb.tile([P, T], F32, name="old_sb")
+        nc.sync.dma_start(old_sb[:], old)
+
+        trust_sb = sb.tile([P, 1], F32, name="trust_sb")
+        nc.gpsimd.dma_start(trust_sb[:], trust)
+        size_col = sb.tile([P, PACK], F32, name="size_col")
+        nc.gpsimd.dma_start(size_col[:], size[0].rearrange("(p c) -> p c", c=PACK))
+        ident = sb.tile([P, P], F32, name="ident")
+        make_identity(nc, ident[:])
+        ntr = sb.tile([P, 1], F32, name="ntr")
+        nc.gpsimd.tensor_scalar(ntr[:], trust_sb[:], -1.0 / PAGE, 0.0, ALU.mult, ALU.add)
+
+        warm = sb.tile([P, 1], F32, name="warm")
+        zero = sb.tile([P, 1], F32, name="zero")
+        nc.vector.memset(zero[:], 0.0)
+        nc.scalar.activation(warm[:], zero[:], ACT.Exp)
+
+        size_ps = ps.tile([P, PACK, P], F32, name="size_ps")
+        for c in range(PACK):
+            nc.tensor.transpose(size_ps[:, c, :], size_col[:, c : c + 1].to_broadcast([P, P]), ident[:])
+
+        def quantise(raw, name):
+            grouped = sb.tile([P, Q, PACK], BF16, name=name + "_bf", align_bytes=64)
+            nc.scalar.copy(grouped[:], raw[:].rearrange("p j w -> p w j"))
+            codes = sb.tile([P, Q], U32, name=name + "_codes", align_bytes=64)
+            scales = sb.tile([P, Q], U8, name=name + "_scales", align_bytes=64)
+            nc.vector.quantize_mx(out=codes[:].bitcast(FP8X4), scales=scales[:], in_=grouped[:].rearrange("p w j -> p (w j)"))
+            return codes, scales
+
+        def half_offsets(h):
+            return offsets[:, h * (HALF // 16) : (h + 1) * (HALF // 16)]
+
+        def product(words, scale_g, row0, codes, scales, name):
+            banks = []
+            for h in range(2):
+                wg = sb.tile([P, HALF], U32, name=name + "_wg%d" % h, align_bytes=64)
+                nc.vector.tensor_copy(wg[:], words[:].bitcast(U32).indirect(half_offsets(h)))
+                bank = ps.tile([P, HALF], F32, name=name + "_bank%d" % h)
+                nc.tensor.matmul_mx(out=bank[:], lhsT=codes[:].bitcast(FP8X4), lhsT_scale=scales[:], rhs=wg[:].bitcast(FP8X4),
+                                    rhs_scale=scale_g[row0:P, h * HALF : (h + 1) * HALF], start=True, stop=True)
+                banks.append(bank)
+            return banks
+
+        ksg = sb.tile([P, I], U8, name="ksg", align_bytes=64)
+        nc.vector.tensor_copy(ksg[:], ks[:].indirect(offsets[:]))
+        q_codes, q_scales = quantise(q_raw, "q")
+        a = product(kw, ksg, 0, q_codes, q_scales, "a")
+        vsg = sb.tile([P, I], U8, name="vsg", align_bytes=64)
+        nc.vector.tensor_copy(vsg[:], vs[:].indirect(offsets[:]))
+
+        asum = sb.tile([P, G], F32, name="asum")
+        b = sb.tile([P, G, PAGE], F32, name="b")
+        for h in range(2):
+            nc.vector.tensor_reduce(asum[:, h * HG : (h + 1) * HG], a[h][:].rearrange("q (g j) -> q g j", j=PAGE), AX.X, ALU.add)
+        for h in range(2):
+            pg = slice(h * HG, (h + 1) * HG)
+            nc.vector.scalar_tensor_tensor(b[:, pg, :], asum[:, pg].unsqueeze(2).to_broadcast([P, HG, PAGE]), ntr[:],
+                                           a[h][:].rearrange("q (g j) -> q g j", j=PAGE), ALU.mult, ALU.add)
+        g_codes, g_scales = quantise(g_raw, "g")
+        nmax = sb.tile([P, 1], F32, name="nmax")
+        nc.vector.tensor_reduce(nmax[:], b[:].rearrange("q g j -> q (g j)"), AX.X, ALU.max, negate=True)
+        p = sb.tile([P, I], F32, name="p")
+        z = sb.tile([P, 1], F32, name="z")
+        nc.scalar.activation(p[:], b[:].rearrange("q g j -> q (g j)"), ACT.Exp, bias=nmax[:], accum_out=z[:])
+
+        c0 = product(vw, vsg, VAL_ROW, g_codes, g_scales, "c")
+        rz = sb.tile([P, 1], F32, name="rz")
+        nc.vector.reciprocal(rz[:], z[:])
+        pzs = sb.tile([P, I], F32, name="pzs")
+        nc.vector.scalar_tensor_tensor(pzs[:].rearrange("q (s c) -> q s c", c=PACK), p[:].rearrange("q (s c) -> q s c", c=PACK), rz[:],
+                                       size_ps[:].rearrange("q c s -> q s c"), ALU.mult, ALU.mult)
+        nu = sb.tile([P, I], F32, name="nu")
+        w = [sb.tile([P, 1], F32, name="w%d" % h) for h in range(2)]
+        for h in range(2):
+            cols = slice(h * HALF, (h + 1) * HALF)
+            nc.vector.scalar_tensor_tensor(nu[:, cols], c0[h][:], -512.0, pzs[:, cols], ALU.mult, ALU.mult, accum_out=w[h][:])
+        dz = sb.tile([P, 1], F32, name="dz")
+        nc.vector.tensor_scalar(dz[:], w[0][:], w[1][:], rz[:], ALU.add, ALU.mult)
+        db = sb.tile([P, I], F32, name="db")
+        for h in range(2):
+            cols = slice(h * HALF, (h + 1) * HALF)
+            nc.vector.scalar_tensor_tensor(db[:, cols], p[:, cols], dz[:], nu[:, cols], ALU.mult, ALU.subtract)
+        dsum = sb.tile([P, G], F32, name="dsum")
+        r1 = sb.tile([P, I], F32, name="r1")
+        for h in range(2):
+            cols = slice(h * HALF, (h + 1) * HALF)
+            pg = slice(h * HG, (h + 1) * HG)
+            nc.vector.tensor_reduce(dsum[:, pg], db[:, cols].rearrange("q (g j) -> q g j", j=PAGE), AX.X, ALU.add)
+            nc.scalar.activation(r1[:, cols].rearrange("q (g j) -> q g j", j=PAGE), dsum[:, pg].unsqueeze(2).to_broadcast([P, HG, PAGE]),
+                                 ACT.Copy, scale=ntr[:])
+        for h in range(2):
+            cols = slice(h * HALF, (h + 1) * HALF)
+            nc.vector.tensor_tensor(gf[:].indirect(half_offsets(h)), db[:, cols], r1[:, cols], ALU.add)
+
+        res = sb.tile([P, T], F32, name="res")
+        t0 = 0
+        for n, width in enumerate(OUT_CHUNKS):
+            cols = slice(t0, t0 + width)
+            nc.vector.tensor_tensor(res[:, cols], gf[:, cols], old_sb[:, cols], ALU.add)
+            (nc.sync if n % 2 == 0 else nc.scalar).dma_start(out[:, cols], res[:, cols])
+            t0 += width

@@ -23,7 +23,7 @@ PAGE = I // G
 HALF = I // 2
 HG = G // 2
 VAL_ROW = 4
-OUT_CHUNKS = [256, 512, 640, 640]
+OUT_CHUNKS = [384, 512, 512, 384, 256]
 
 
 def tile_attend_bpagecentred_s_kernel(tc, query, keys_words, keys_scales, trust, gout, vals_words, vals_scales, size, old, offs, out):
@@ -35,7 +35,7 @@ def tile_attend_bpagecentred_s_kernel(tc, query, keys_words, keys_scales, trust,
         offsets = sb.tile([P, I // 16], U16, name="offsets")
         nc.sync.dma_start(offsets[:], offs)
 
-        ks = sb.tile([P, T], U8, name="ks", align_bytes=64)
+        ks = sb.tile([P, T], U8, name="ks", tag="ks_vw", align_bytes=64)
         vs = sb.tile([P, T], U8, name="vs", align_bytes=64)
         gf = sb.tile([P, T], F32, name="gf", align_bytes=64)
         nc.vector.memset(ks[:].bitcast(I32), 0)
@@ -45,18 +45,12 @@ def tile_attend_bpagecentred_s_kernel(tc, query, keys_words, keys_scales, trust,
         for r in range(4):
             nc.scalar.dma_start(ks[32 * r : 32 * r + 4, :].bitcast(I32), keys_scales[0, 4 * r : 4 * r + 4, :].bitcast(I32))
 
-        q_raw = sb.tile([P, PACK, Q], F32, name="q_raw")
+        q_raw = sb.tile([P, PACK, Q], F32, name="q_raw", tag="raw")
         nc.sync.dma_start(q_raw[:], query.rearrange("(p j) w -> p j w", j=PACK))
-        kw = sb.tile([P, T], I32, name="kw", align_bytes=64)
+        kw = sb.tile([P, T], I32, name="kw", tag="kw_old", align_bytes=64)
         nc.sync.dma_start(kw[:], keys_words[0].rearrange("p n t -> p (n t)").bitcast(I32))
         for r in range(4):
             nc.sync.dma_start(vs[32 * r + VAL_ROW : 32 * r + VAL_ROW + 4, :].bitcast(I32), vals_scales[0, 4 * r : 4 * r + 4, :].bitcast(I32))
-        g_raw = sb.tile([P, PACK, Q], F32, name="g_raw")
-        nc.sync.dma_start(g_raw[:], gout.rearrange("(p j) w -> p j w", j=PACK))
-        vw = sb.tile([P, T], I32, name="vw", align_bytes=64)
-        nc.sync.dma_start(vw[:], vals_words[0].rearrange("p n t -> p (n t)").bitcast(I32))
-        old_sb = sb.tile([P, T], F32, name="old_sb")
-        nc.sync.dma_start(old_sb[:], old)
 
         trust_sb = sb.tile([P, 1], F32, name="trust_sb")
         nc.gpsimd.dma_start(trust_sb[:], trust)
@@ -64,17 +58,9 @@ def tile_attend_bpagecentred_s_kernel(tc, query, keys_words, keys_scales, trust,
         nc.gpsimd.dma_start(size_col[:], size[0].rearrange("(p c) -> p c", c=PACK))
         ident = sb.tile([P, P], F32, name="ident")
         make_identity(nc, ident[:])
-        ntr = sb.tile([P, 1], F32, name="ntr")
-        nc.gpsimd.tensor_scalar(ntr[:], trust_sb[:], -1.0 / PAGE, 0.0, ALU.mult, ALU.add)
 
         warm = sb.tile([P, 1], F32, name="warm")
-        zero = sb.tile([P, 1], F32, name="zero")
-        nc.vector.memset(zero[:], 0.0)
-        nc.scalar.activation(warm[:], zero[:], ACT.Exp)
-
-        size_ps = ps.tile([P, PACK, P], F32, name="size_ps")
-        for c in range(PACK):
-            nc.tensor.transpose(size_ps[:, c, :], size_col[:, c : c + 1].to_broadcast([P, P]), ident[:])
+        nc.scalar.activation(warm[:], q_raw[:, 0, 0:1], ACT.Exp, scale=0.0)
 
         def quantise(raw, name):
             grouped = sb.tile([P, Q, PACK], BF16, name=name + "_bf", align_bytes=64)
@@ -90,9 +76,9 @@ def tile_attend_bpagecentred_s_kernel(tc, query, keys_words, keys_scales, trust,
         def product(words, scale_g, row0, codes, scales, name):
             banks = []
             for h in range(2):
-                wg = sb.tile([P, HALF], U32, name=name + "_wg%d" % h, align_bytes=64)
+                wg = sb.tile([P, HALF], U32, name=name + "_wg%d" % h, tag=name + "_wg%d" % h, align_bytes=64)
                 nc.vector.tensor_copy(wg[:], words[:].bitcast(U32).indirect(half_offsets(h)))
-                bank = ps.tile([P, HALF], F32, name=name + "_bank%d" % h)
+                bank = ps.tile([P, HALF], F32, name=name + "_bank%d" % h, tag=name + "_bank%d" % h)
                 nc.tensor.matmul_mx(out=bank[:], lhsT=codes[:].bitcast(FP8X4), lhsT_scale=scales[:], rhs=wg[:].bitcast(FP8X4),
                                     rhs_scale=scale_g[row0:P, h * HALF : (h + 1) * HALF], start=True, stop=True)
                 banks.append(bank)
@@ -100,8 +86,16 @@ def tile_attend_bpagecentred_s_kernel(tc, query, keys_words, keys_scales, trust,
 
         ksg = sb.tile([P, I], U8, name="ksg", align_bytes=64)
         nc.vector.tensor_copy(ksg[:], ks[:].indirect(offsets[:]))
+        vw = sb.tile([P, T], I32, name="vw", tag="ks_vw", align_bytes=64)
+        nc.sync.dma_start(vw[:], vals_words[0].rearrange("p n t -> p (n t)").bitcast(I32))
         q_codes, q_scales = quantise(q_raw, "q")
+        g_raw = sb.tile([P, PACK, Q], F32, name="g_raw", tag="raw")
+        nc.scalar.dma_start(g_raw[:], gout.rearrange("(p j) w -> p j w", j=PACK))
+        ntr = sb.tile([P, 1], F32, name="ntr")
+        nc.scalar.activation(ntr[:], trust_sb[:], ACT.Copy, scale=-1.0 / PAGE)
         a = product(kw, ksg, 0, q_codes, q_scales, "a")
+        old_sb = sb.tile([P, T], F32, name="old_sb", tag="kw_old", align_bytes=64)
+        nc.sync.dma_start(old_sb[:], old)
         vsg = sb.tile([P, I], U8, name="vsg", align_bytes=64)
         nc.vector.tensor_copy(vsg[:], vs[:].indirect(offsets[:]))
 
@@ -113,9 +107,14 @@ def tile_attend_bpagecentred_s_kernel(tc, query, keys_words, keys_scales, trust,
             pg = slice(h * HG, (h + 1) * HG)
             nc.vector.scalar_tensor_tensor(b[:, pg, :], asum[:, pg].unsqueeze(2).to_broadcast([P, HG, PAGE]), ntr[:],
                                            a[h][:].rearrange("q (g j) -> q g j", j=PAGE), ALU.mult, ALU.add)
+        size_ps = ps.tile([P, PACK, P], F32, name="size_ps", tag="a_bank0")
+        for c in range(PACK):
+            nc.tensor.transpose(size_ps[:, c, :], size_col[:, c : c + 1].to_broadcast([P, P]), ident[:])
+
         g_codes, g_scales = quantise(g_raw, "g")
         nmax = sb.tile([P, 1], F32, name="nmax")
-        nc.vector.tensor_reduce(nmax[:], b[:].rearrange("q g j -> q (g j)"), AX.X, ALU.max, negate=True)
+        negb = sb.tile([P, I], F32, name="negb", tag="c_wg0", align_bytes=64)
+        nc.vector.tensor_scalar(negb[:], b[:].rearrange("q g j -> q (g j)"), -1.0, None, ALU.mult, ALU.min, accum_out=nmax[:])
         p = sb.tile([P, I], F32, name="p")
         z = sb.tile([P, 1], F32, name="z")
         nc.scalar.activation(p[:], b[:].rearrange("q g j -> q (g j)"), ACT.Exp, bias=nmax[:], accum_out=z[:])
@@ -139,15 +138,15 @@ def tile_attend_bpagecentred_s_kernel(tc, query, keys_words, keys_scales, trust,
             nc.vector.scalar_tensor_tensor(db[:, cols], p[:, cols], dz[:], nu[:, cols], ALU.mult, ALU.subtract)
         dsum = sb.tile([P, G], F32, name="dsum")
         r1 = sb.tile([P, I], F32, name="r1")
-        for h in range(2):
-            cols = slice(h * HALF, (h + 1) * HALF)
-            pg = slice(h * HG, (h + 1) * HG)
-            nc.vector.tensor_reduce(dsum[:, pg], db[:, cols].rearrange("q (g j) -> q g j", j=PAGE), AX.X, ALU.add)
-            nc.scalar.activation(r1[:, cols].rearrange("q (g j) -> q g j", j=PAGE), dsum[:, pg].unsqueeze(2).to_broadcast([P, HG, PAGE]),
+        pieces = [(0, 8), (8, 32)]
+        for g0, g1 in pieces:
+            cols = slice(g0 * PAGE, g1 * PAGE)
+            nc.vector.tensor_reduce(dsum[:, g0:g1], db[:, cols].rearrange("q (g j) -> q g j", j=PAGE), AX.X, ALU.add)
+            nc.scalar.activation(r1[:, cols].rearrange("q (g j) -> q g j", j=PAGE), dsum[:, g0:g1].unsqueeze(2).to_broadcast([P, g1 - g0, PAGE]),
                                  ACT.Copy, scale=ntr[:])
-        for h in range(2):
-            cols = slice(h * HALF, (h + 1) * HALF)
-            nc.vector.tensor_tensor(gf[:].indirect(half_offsets(h)), db[:, cols], r1[:, cols], ALU.add)
+        for g0, g1 in pieces:
+            cols = slice(g0 * PAGE, g1 * PAGE)
+            nc.vector.tensor_tensor(gf[:].indirect(offsets[:, g0:g1]), db[:, cols], r1[:, cols], ALU.add)
 
         res = sb.tile([P, T], F32, name="res")
         t0 = 0

@@ -35,37 +35,38 @@ def tile_attend_bpagecentred_s_kernel(tc, query, keys_words, keys_scales, trust,
         offsets = sb.tile([P, I // 16], U16, name="offsets")
         nc.sync.dma_start(offsets[:], offs)
 
+        q_raw = sb.tile([P, PACK, Q], F32, name="q_raw", tag="raw")
+        nc.sync.dma_start(q_raw[:], query.rearrange("(p j) w -> p j w", j=PACK))
+        trust_sb = sb.tile([P, 1], F32, name="trust_sb")
+        nc.sync.dma_start(trust_sb[:], trust)
+
         ks = sb.tile([P, T], U8, name="ks", tag="ks_vw", align_bytes=64)
         vs = sb.tile([P, T], U8, name="vs", align_bytes=64)
         gf = sb.tile([P, T], F32, name="gf", align_bytes=64)
-        nc.vector.memset(ks[:].bitcast(I32), 0)
+        nc.vector.memset(ks[:, : T // 2].bitcast(I32), 0)
+        nc.gpsimd.memset(ks[:, T // 2 :].bitcast(I32), 0)
         nc.vector.memset(vs[:].bitcast(I32), 0)
         nc.vector.memset(gf[:], 0.0)
-
         for r in range(4):
-            nc.scalar.dma_start(ks[32 * r : 32 * r + 4, :].bitcast(I32), keys_scales[0, 4 * r : 4 * r + 4, :].bitcast(I32))
-
-        q_raw = sb.tile([P, PACK, Q], F32, name="q_raw", tag="raw")
-        nc.sync.dma_start(q_raw[:], query.rearrange("(p j) w -> p j w", j=PACK))
+            nc.sync.dma_start(ks[32 * r : 32 * r + 4, :].bitcast(I32), keys_scales[0, 4 * r : 4 * r + 4, :].bitcast(I32))
         kw = sb.tile([P, T], I32, name="kw", tag="kw_old", align_bytes=64)
         nc.sync.dma_start(kw[:], keys_words[0].rearrange("p n t -> p (n t)").bitcast(I32))
         for r in range(4):
             nc.sync.dma_start(vs[32 * r + VAL_ROW : 32 * r + VAL_ROW + 4, :].bitcast(I32), vals_scales[0, 4 * r : 4 * r + 4, :].bitcast(I32))
 
-        trust_sb = sb.tile([P, 1], F32, name="trust_sb")
-        nc.gpsimd.dma_start(trust_sb[:], trust)
         size_col = sb.tile([P, PACK], F32, name="size_col")
         nc.gpsimd.dma_start(size_col[:], size[0].rearrange("(p c) -> p c", c=PACK))
         ident = sb.tile([P, P], F32, name="ident")
         make_identity(nc, ident[:])
-
+        ntr = sb.tile([P, 1], F32, name="ntr")
+        nc.gpsimd.tensor_scalar(ntr[:], trust_sb[:], -1.0 / PAGE, 0.0, ALU.mult, ALU.add)
         warm = sb.tile([P, 1], F32, name="warm")
         nc.scalar.activation(warm[:], q_raw[:, 0, 0:1], ACT.Exp, scale=0.0)
 
         def quantise(raw, name):
             grouped = sb.tile([P, Q, PACK], BF16, name=name + "_bf", align_bytes=64)
             nc.scalar.copy(grouped[:], raw[:].rearrange("p j w -> p w j"))
-            codes = sb.tile([P, Q], U32, name=name + "_codes", align_bytes=64)
+            codes = sb.tile([P, Q], U32, name=name + "_codes", tag="codes", align_bytes=64)
             scales = sb.tile([P, Q], U8, name=name + "_scales", align_bytes=64)
             nc.vector.quantize_mx(out=codes[:].bitcast(FP8X4), scales=scales[:], in_=grouped[:].rearrange("p w j -> p (w j)"))
             return codes, scales
@@ -73,16 +74,12 @@ def tile_attend_bpagecentred_s_kernel(tc, query, keys_words, keys_scales, trust,
         def half_offsets(h):
             return offsets[:, h * (HALF // 16) : (h + 1) * (HALF // 16)]
 
-        def product(words, scale_g, row0, codes, scales, name):
-            banks = []
+        def product(words, scale_g, row0, codes, scales, name, banks):
             for h in range(2):
-                wg = sb.tile([P, HALF], U32, name=name + "_wg%d" % h, tag=name + "_wg%d" % h, align_bytes=64)
+                wg = sb.tile([P, HALF], U32, name=name + "_wg%d" % h, tag=(name + "_wg0" if h == 0 else "wg1"), align_bytes=64)
                 nc.vector.tensor_copy(wg[:], words[:].bitcast(U32).indirect(half_offsets(h)))
-                bank = ps.tile([P, HALF], F32, name=name + "_bank%d" % h, tag=name + "_bank%d" % h)
-                nc.tensor.matmul_mx(out=bank[:], lhsT=codes[:].bitcast(FP8X4), lhsT_scale=scales[:], rhs=wg[:].bitcast(FP8X4),
+                nc.tensor.matmul_mx(out=banks[h], lhsT=codes[:].bitcast(FP8X4), lhsT_scale=scales[:], rhs=wg[:].bitcast(FP8X4),
                                     rhs_scale=scale_g[row0:P, h * HALF : (h + 1) * HALF], start=True, stop=True)
-                banks.append(bank)
-            return banks
 
         ksg = sb.tile([P, I], U8, name="ksg", align_bytes=64)
         nc.vector.tensor_copy(ksg[:], ks[:].indirect(offsets[:]))
@@ -91,9 +88,8 @@ def tile_attend_bpagecentred_s_kernel(tc, query, keys_words, keys_scales, trust,
         q_codes, q_scales = quantise(q_raw, "q")
         g_raw = sb.tile([P, PACK, Q], F32, name="g_raw", tag="raw")
         nc.scalar.dma_start(g_raw[:], gout.rearrange("(p j) w -> p j w", j=PACK))
-        ntr = sb.tile([P, 1], F32, name="ntr")
-        nc.scalar.activation(ntr[:], trust_sb[:], ACT.Copy, scale=-1.0 / PAGE)
-        a = product(kw, ksg, 0, q_codes, q_scales, "a")
+        a = [ps.tile([P, HALF], F32, name="a_bank%d" % h, tag="a_bank%d" % h) for h in range(2)]
+        product(kw, ksg, 0, q_codes, q_scales, "a", [a[0][:], a[1][:]])
         old_sb = sb.tile([P, T], F32, name="old_sb", tag="kw_old", align_bytes=64)
         nc.sync.dma_start(old_sb[:], old)
         vsg = sb.tile([P, I], U8, name="vsg", align_bytes=64)
@@ -119,26 +115,26 @@ def tile_attend_bpagecentred_s_kernel(tc, query, keys_words, keys_scales, trust,
         z = sb.tile([P, 1], F32, name="z")
         nc.scalar.activation(p[:], b[:].rearrange("q g j -> q (g j)"), ACT.Exp, bias=nmax[:], accum_out=z[:])
 
-        c0 = product(vw, vsg, VAL_ROW, g_codes, g_scales, "c")
-        rz = sb.tile([P, 1], F32, name="rz")
-        nc.vector.reciprocal(rz[:], z[:])
-        pzs = sb.tile([P, I], F32, name="pzs")
-        nc.vector.scalar_tensor_tensor(pzs[:].rearrange("q (s c) -> q s c", c=PACK), p[:].rearrange("q (s c) -> q s c", c=PACK), rz[:],
+        pieces = [(0, 8), (8, 32)]
+        c0 = ps.tile([P, I], F32, name="c0")
+        product(vw, vsg, VAL_ROW, g_codes, g_scales, "c", [c0[:, :HALF], c0[:, HALF:]])
+        late = sb.tile([P, I + 8], F32, name="late", tag="ks_vw", align_bytes=64)
+        ps_size = late[:, :I]
+        rz = late[:, I : I + 1]
+        nc.vector.reciprocal(rz, z[:])
+        nc.vector.scalar_tensor_tensor(ps_size.rearrange("q (s c) -> q s c", c=PACK), p[:].rearrange("q (s c) -> q s c", c=PACK), -512.0,
                                        size_ps[:].rearrange("q c s -> q s c"), ALU.mult, ALU.mult)
+        pn = sb.tile([P, I], F32, name="pn")
+        nc.scalar.activation(pn[:], p[:], ACT.Copy, scale=rz)
         nu = sb.tile([P, I], F32, name="nu")
-        w = [sb.tile([P, 1], F32, name="w%d" % h) for h in range(2)]
-        for h in range(2):
-            cols = slice(h * HALF, (h + 1) * HALF)
-            nc.vector.scalar_tensor_tensor(nu[:, cols], c0[h][:], -512.0, pzs[:, cols], ALU.mult, ALU.mult, accum_out=w[h][:])
-        dz = sb.tile([P, 1], F32, name="dz")
-        nc.vector.tensor_scalar(dz[:], w[0][:], w[1][:], rz[:], ALU.add, ALU.mult)
+        w = sb.tile([P, 1], F32, name="w")
+        nc.vector.scalar_tensor_tensor(nu[:], c0[:], rz, ps_size, ALU.mult, ALU.mult, accum_out=w[:])
         db = sb.tile([P, I], F32, name="db")
-        for h in range(2):
-            cols = slice(h * HALF, (h + 1) * HALF)
-            nc.vector.scalar_tensor_tensor(db[:, cols], p[:, cols], dz[:], nu[:, cols], ALU.mult, ALU.subtract)
+        for g0, g1 in pieces:
+            cols = slice(g0 * PAGE, g1 * PAGE)
+            nc.vector.scalar_tensor_tensor(db[:, cols], pn[:, cols], w[:], nu[:, cols], ALU.mult, ALU.subtract)
         dsum = sb.tile([P, G], F32, name="dsum")
         r1 = sb.tile([P, I], F32, name="r1")
-        pieces = [(0, 8), (8, 32)]
         for g0, g1 in pieces:
             cols = slice(g0 * PAGE, g1 * PAGE)
             nc.vector.tensor_reduce(dsum[:, g0:g1], db[:, cols].rearrange("q (g j) -> q g j", j=PAGE), AX.X, ALU.add)

@@ -23,7 +23,7 @@ PAGE = I // G
 HALF = I // 2
 HG = G // 2
 VAL_ROW = 4
-OUT_CHUNKS = [384, 512, 512, 384, 256]
+OUT_CHUNKS = [448, 448, 448, 384, 320]
 
 
 def tile_attend_bpagecentred_s_kernel(tc, query, keys_words, keys_scales, trust, gout, vals_words, vals_scales, size, old, offs, out):
@@ -64,7 +64,7 @@ def tile_attend_bpagecentred_s_kernel(tc, query, keys_words, keys_scales, trust,
         nc.scalar.activation(warm[:], q_raw[:, 0, 0:1], ACT.Exp, scale=0.0)
 
         def quantise(raw, name):
-            grouped = sb.tile([P, Q, PACK], BF16, name=name + "_bf", align_bytes=64)
+            grouped = sb.tile([P, Q, PACK], BF16, name=name + "_bf", tag=name + "_bf", align_bytes=64)
             nc.scalar.copy(grouped[:], raw[:].rearrange("p j w -> p w j"))
             codes = sb.tile([P, Q], U32, name=name + "_codes", tag="codes", align_bytes=64)
             scales = sb.tile([P, Q], U8, name=name + "_scales", align_bytes=64)
@@ -74,12 +74,12 @@ def tile_attend_bpagecentred_s_kernel(tc, query, keys_words, keys_scales, trust,
         def half_offsets(h):
             return offsets[:, h * (HALF // 16) : (h + 1) * (HALF // 16)]
 
-        def product(words, scale_g, row0, codes, scales, name, banks):
+        def product(words, scale_g, row0, codes, scales, name, banks, tags):
             for h in range(2):
-                wg = sb.tile([P, HALF], U32, name=name + "_wg%d" % h, tag=(name + "_wg0" if h == 0 else "wg1"), align_bytes=64)
+                wg = sb.tile([P, HALF], U32, name=name + "_wg%d" % h, tag=tags[h], align_bytes=64)
                 nc.vector.tensor_copy(wg[:], words[:].bitcast(U32).indirect(half_offsets(h)))
                 nc.tensor.matmul_mx(out=banks[h], lhsT=codes[:].bitcast(FP8X4), lhsT_scale=scales[:], rhs=wg[:].bitcast(FP8X4),
-                                    rhs_scale=scale_g[row0:P, h * HALF : (h + 1) * HALF], start=True, stop=True)
+                                    rhs_scale=scale_g[h][row0:P, :], start=True, stop=True)
 
         ksg = sb.tile([P, I], U8, name="ksg", align_bytes=64)
         nc.vector.tensor_copy(ksg[:], ks[:].indirect(offsets[:]))
@@ -89,11 +89,11 @@ def tile_attend_bpagecentred_s_kernel(tc, query, keys_words, keys_scales, trust,
         g_raw = sb.tile([P, PACK, Q], F32, name="g_raw", tag="raw")
         nc.scalar.dma_start(g_raw[:], gout.rearrange("(p j) w -> p j w", j=PACK))
         a = [ps.tile([P, HALF], F32, name="a_bank%d" % h, tag="a_bank%d" % h) for h in range(2)]
-        product(kw, ksg, 0, q_codes, q_scales, "a", [a[0][:], a[1][:]])
+        product(kw, [ksg[:, :HALF], ksg[:, HALF:]], 0, q_codes, q_scales, "a", [a[0][:], a[1][:]], ["a_wg0", "wg1"])
         old_sb = sb.tile([P, T], F32, name="old_sb", tag="kw_old", align_bytes=64)
         nc.sync.dma_start(old_sb[:], old)
-        vsg = sb.tile([P, I], U8, name="vsg", align_bytes=64)
-        nc.vector.tensor_copy(vsg[:], vs[:].indirect(offsets[:]))
+        vsg0 = sb.tile([P, HALF], U8, name="vsg0", align_bytes=64)
+        nc.vector.tensor_copy(vsg0[:], vs[:].indirect(half_offsets(0)))
 
         asum = sb.tile([P, G], F32, name="asum")
         b = sb.tile([P, G, PAGE], F32, name="b")
@@ -107,23 +107,27 @@ def tile_attend_bpagecentred_s_kernel(tc, query, keys_words, keys_scales, trust,
         for c in range(PACK):
             nc.tensor.transpose(size_ps[:, c, :], size_col[:, c : c + 1].to_broadcast([P, P]), ident[:])
 
+        nsize = sb.tile([P, I], F32, name="nsize")
+        nc.scalar.activation(nsize[:].rearrange("q (s c) -> q s c", c=PACK), size_ps[:].rearrange("q c s -> q s c"), ACT.Copy, scale=-512.0)
         g_codes, g_scales = quantise(g_raw, "g")
         nmax = sb.tile([P, 1], F32, name="nmax")
-        negb = sb.tile([P, I], F32, name="negb", tag="c_wg0", align_bytes=64)
+        negb = sb.tile([P, I], F32, name="negb", tag="negb_vsg", align_bytes=64)
         nc.vector.tensor_scalar(negb[:], b[:].rearrange("q g j -> q (g j)"), -1.0, None, ALU.mult, ALU.min, accum_out=nmax[:])
+        vsg1 = sb.tile([P, HALF], U8, name="vsg1", tag="negb_vsg", align_bytes=64)
+        nc.vector.tensor_copy(vsg1[:], vs[:].indirect(half_offsets(1)))
         p = sb.tile([P, I], F32, name="p")
         z = sb.tile([P, 1], F32, name="z")
         nc.scalar.activation(p[:], b[:].rearrange("q g j -> q (g j)"), ACT.Exp, bias=nmax[:], accum_out=z[:])
 
         pieces = [(0, 8), (8, 32)]
         c0 = ps.tile([P, I], F32, name="c0")
-        product(vw, vsg, VAL_ROW, g_codes, g_scales, "c", [c0[:, :HALF], c0[:, HALF:]])
-        late = sb.tile([P, I + 8], F32, name="late", tag="ks_vw", align_bytes=64)
-        ps_size = late[:, :I]
-        rz = late[:, I : I + 1]
+        product(vw, [vsg0[:], vsg1[:]], VAL_ROW, g_codes, g_scales, "c", [c0[:, :HALF], c0[:, HALF:]], ["g_bf", "wg1"])
+        late = sb.tile([P, I], F32, name="late")
+        ps_size = late[:]
+        rz_t = sb.tile([P, 1], F32, name="rz_t", tag="g_bf", align_bytes=64)
+        rz = rz_t[:]
         nc.vector.reciprocal(rz, z[:])
-        nc.vector.scalar_tensor_tensor(ps_size.rearrange("q (s c) -> q s c", c=PACK), p[:].rearrange("q (s c) -> q s c", c=PACK), -512.0,
-                                       size_ps[:].rearrange("q c s -> q s c"), ALU.mult, ALU.mult)
+        nc.gpsimd.tensor_tensor(ps_size, p[:], nsize[:], ALU.mult)
         pn = sb.tile([P, I], F32, name="pn")
         nc.scalar.activation(pn[:], p[:], ACT.Copy, scale=rz)
         nu = sb.tile([P, I], F32, name="nu")

@@ -19,10 +19,14 @@ AX = mybir.AxisListType
 
 P = 128
 PACK = 4
+QUADRANTS = 4
 PAGE = I // G
 HALF = I // 2
-HG = G // 2
-VAL_ROW = 4
+HALF_PAGES = G // 2
+GRAD_SCALE = 512.0
+KEY_FIRST_ROW = 0
+VAL_FIRST_ROW = 4
+SCATTER_PAGES = [(0, 8), (8, G)]
 OUT_CHUNKS = [448, 448, 448, 384, 320]
 
 
@@ -47,21 +51,26 @@ def tile_attend_bpagecentred_s_kernel(tc, query, keys_words, keys_scales, trust,
         nc.gpsimd.memset(ks[:, T // 2 :].bitcast(I32), 0)
         nc.vector.memset(vs[:].bitcast(I32), 0)
         nc.vector.memset(gf[:], 0.0)
-        for r in range(4):
-            nc.sync.dma_start(ks[32 * r : 32 * r + 4, :].bitcast(I32), keys_scales[0, 4 * r : 4 * r + 4, :].bitcast(I32))
+
+        def load_scale_rows(plane, scales, first_row):
+            for z in range(QUADRANTS):
+                row = 32 * z + first_row
+                nc.sync.dma_start(plane[row : row + 4, :].bitcast(I32), scales[0, 4 * z : 4 * z + 4, :].bitcast(I32))
+
+        def load_words(tile, words):
+            nc.sync.dma_start(tile[:], words[0].rearrange("p n t -> p (n t)").bitcast(I32))
+
+        load_scale_rows(ks, keys_scales, KEY_FIRST_ROW)
         kw = sb.tile([P, T], I32, name="kw", tag="kw_old", align_bytes=64)
-        nc.sync.dma_start(kw[:], keys_words[0].rearrange("p n t -> p (n t)").bitcast(I32))
-        for r in range(4):
-            nc.sync.dma_start(vs[32 * r + VAL_ROW : 32 * r + VAL_ROW + 4, :].bitcast(I32), vals_scales[0, 4 * r : 4 * r + 4, :].bitcast(I32))
+        load_words(kw, keys_words)
+        load_scale_rows(vs, vals_scales, VAL_FIRST_ROW)
 
         size_col = sb.tile([P, PACK], F32, name="size_col")
         nc.gpsimd.dma_start(size_col[:], size[0].rearrange("(p c) -> p c", c=PACK))
         ident = sb.tile([P, P], F32, name="ident")
         make_identity(nc, ident[:])
-        ntr = sb.tile([P, 1], F32, name="ntr")
-        nc.gpsimd.tensor_scalar(ntr[:], trust_sb[:], -1.0 / PAGE, 0.0, ALU.mult, ALU.add)
-        warm = sb.tile([P, 1], F32, name="warm")
-        nc.scalar.activation(warm[:], q_raw[:, 0, 0:1], ACT.Exp, scale=0.0)
+        centre = sb.tile([P, 1], F32, name="centre")
+        nc.gpsimd.tensor_scalar(centre[:], trust_sb[:], -1.0 / PAGE, 0.0, ALU.mult, ALU.add)
 
         def quantise(raw, name):
             grouped = sb.tile([P, Q, PACK], BF16, name=name + "_bf", tag=name + "_bf", align_bytes=64)
@@ -74,22 +83,25 @@ def tile_attend_bpagecentred_s_kernel(tc, query, keys_words, keys_scales, trust,
         def half_offsets(h):
             return offsets[:, h * (HALF // 16) : (h + 1) * (HALF // 16)]
 
-        def product(words, scale_g, row0, codes, scales, name, banks, tags):
+        def product(words, gathered_scales, first_row, codes, scales, name, results, tags):
             for h in range(2):
-                wg = sb.tile([P, HALF], U32, name=name + "_wg%d" % h, tag=tags[h], align_bytes=64)
-                nc.vector.tensor_copy(wg[:], words[:].bitcast(U32).indirect(half_offsets(h)))
-                nc.tensor.matmul_mx(out=banks[h], lhsT=codes[:].bitcast(FP8X4), lhsT_scale=scales[:], rhs=wg[:].bitcast(FP8X4),
-                                    rhs_scale=scale_g[h][row0:P, :], start=True, stop=True)
+                gathered = sb.tile([P, HALF], U32, name=name + "_wg%d" % h, tag=tags[h], align_bytes=64)
+                nc.vector.tensor_copy(gathered[:], words[:].bitcast(U32).indirect(half_offsets(h)))
+                nc.tensor.matmul_mx(out=results[h], lhsT=codes[:].bitcast(FP8X4), lhsT_scale=scales[:], rhs=gathered[:].bitcast(FP8X4),
+                                    rhs_scale=gathered_scales[h][first_row:P, :], start=True, stop=True)
+
+        def by_page(ap):
+            return ap.rearrange("q (g j) -> q g j", j=PAGE)
 
         ksg = sb.tile([P, I], U8, name="ksg", align_bytes=64)
         nc.vector.tensor_copy(ksg[:], ks[:].indirect(offsets[:]))
         vw = sb.tile([P, T], I32, name="vw", tag="ks_vw", align_bytes=64)
-        nc.sync.dma_start(vw[:], vals_words[0].rearrange("p n t -> p (n t)").bitcast(I32))
+        load_words(vw, vals_words)
         q_codes, q_scales = quantise(q_raw, "q")
         g_raw = sb.tile([P, PACK, Q], F32, name="g_raw", tag="raw")
         nc.scalar.dma_start(g_raw[:], gout.rearrange("(p j) w -> p j w", j=PACK))
         a = [ps.tile([P, HALF], F32, name="a_bank%d" % h, tag="a_bank%d" % h) for h in range(2)]
-        product(kw, [ksg[:, :HALF], ksg[:, HALF:]], 0, q_codes, q_scales, "a", [a[0][:], a[1][:]], ["a_wg0", "wg1"])
+        product(kw, [ksg[:, :HALF], ksg[:, HALF:]], KEY_FIRST_ROW, q_codes, q_scales, "a", [a[0][:], a[1][:]], ["a_wg0", "wg1"])
         old_sb = sb.tile([P, T], F32, name="old_sb", tag="kw_old", align_bytes=64)
         nc.sync.dma_start(old_sb[:], old)
         vsg0 = sb.tile([P, HALF], U8, name="vsg0", align_bytes=64)
@@ -98,18 +110,20 @@ def tile_attend_bpagecentred_s_kernel(tc, query, keys_words, keys_scales, trust,
         asum = sb.tile([P, G], F32, name="asum")
         b = sb.tile([P, G, PAGE], F32, name="b")
         for h in range(2):
-            nc.vector.tensor_reduce(asum[:, h * HG : (h + 1) * HG], a[h][:].rearrange("q (g j) -> q g j", j=PAGE), AX.X, ALU.add)
+            nc.vector.tensor_reduce(asum[:, h * HALF_PAGES : (h + 1) * HALF_PAGES], by_page(a[h][:]), AX.X, ALU.add)
         for h in range(2):
-            pg = slice(h * HG, (h + 1) * HG)
-            nc.vector.scalar_tensor_tensor(b[:, pg, :], asum[:, pg].unsqueeze(2).to_broadcast([P, HG, PAGE]), ntr[:],
-                                           a[h][:].rearrange("q (g j) -> q g j", j=PAGE), ALU.mult, ALU.add)
+            pages = slice(h * HALF_PAGES, (h + 1) * HALF_PAGES)
+            nc.vector.scalar_tensor_tensor(b[:, pages, :], asum[:, pages].unsqueeze(2).to_broadcast([P, HALF_PAGES, PAGE]), centre[:],
+                                           by_page(a[h][:]), ALU.mult, ALU.add)
+
         size_ps = ps.tile([P, PACK, P], F32, name="size_ps", tag="a_bank0")
         for c in range(PACK):
             nc.tensor.transpose(size_ps[:, c, :], size_col[:, c : c + 1].to_broadcast([P, P]), ident[:])
 
         nsize = sb.tile([P, I], F32, name="nsize")
-        nc.scalar.activation(nsize[:].rearrange("q (s c) -> q s c", c=PACK), size_ps[:].rearrange("q c s -> q s c"), ACT.Copy, scale=-512.0)
+        nc.scalar.activation(nsize[:].rearrange("q (s c) -> q s c", c=PACK), size_ps[:].rearrange("q c s -> q s c"), ACT.Copy, scale=-GRAD_SCALE)
         g_codes, g_scales = quantise(g_raw, "g")
+
         nmax = sb.tile([P, 1], F32, name="nmax")
         negb = sb.tile([P, I], F32, name="negb", tag="negb_vsg", align_bytes=64)
         nc.vector.tensor_scalar(negb[:], b[:].rearrange("q g j -> q (g j)"), -1.0, None, ALU.mult, ALU.min, accum_out=nmax[:])
@@ -119,39 +133,38 @@ def tile_attend_bpagecentred_s_kernel(tc, query, keys_words, keys_scales, trust,
         z = sb.tile([P, 1], F32, name="z")
         nc.scalar.activation(p[:], b[:].rearrange("q g j -> q (g j)"), ACT.Exp, bias=nmax[:], accum_out=z[:])
 
-        pieces = [(0, 8), (8, 32)]
         c0 = ps.tile([P, I], F32, name="c0")
-        product(vw, [vsg0[:], vsg1[:]], VAL_ROW, g_codes, g_scales, "c", [c0[:, :HALF], c0[:, HALF:]], ["g_bf", "wg1"])
-        late = sb.tile([P, I], F32, name="late")
-        ps_size = late[:]
-        rz_t = sb.tile([P, 1], F32, name="rz_t", tag="g_bf", align_bytes=64)
-        rz = rz_t[:]
-        nc.vector.reciprocal(rz, z[:])
-        nc.gpsimd.tensor_tensor(ps_size, p[:], nsize[:], ALU.mult)
+        product(vw, [vsg0[:], vsg1[:]], VAL_FIRST_ROW, g_codes, g_scales, "c", [c0[:, :HALF], c0[:, HALF:]], ["g_bf", "wg1"])
+        p_nsize = sb.tile([P, I], F32, name="p_nsize")
+        rz = sb.tile([P, 1], F32, name="rz", tag="g_bf", align_bytes=64)
+        nc.vector.reciprocal(rz[:], z[:])
+        nc.gpsimd.tensor_tensor(p_nsize[:], p[:], nsize[:], ALU.mult)
         pn = sb.tile([P, I], F32, name="pn")
-        nc.scalar.activation(pn[:], p[:], ACT.Copy, scale=rz)
+        nc.scalar.activation(pn[:], p[:], ACT.Copy, scale=rz[:])
+
         nu = sb.tile([P, I], F32, name="nu")
         w = sb.tile([P, 1], F32, name="w")
-        nc.vector.scalar_tensor_tensor(nu[:], c0[:], rz, ps_size, ALU.mult, ALU.mult, accum_out=w[:])
+        nc.vector.scalar_tensor_tensor(nu[:], c0[:], rz[:], p_nsize[:], ALU.mult, ALU.mult, accum_out=w[:])
         db = sb.tile([P, I], F32, name="db")
-        for g0, g1 in pieces:
-            cols = slice(g0 * PAGE, g1 * PAGE)
-            nc.vector.scalar_tensor_tensor(db[:, cols], pn[:, cols], w[:], nu[:, cols], ALU.mult, ALU.subtract)
+        for g0, g1 in SCATTER_PAGES:
+            slots = slice(g0 * PAGE, g1 * PAGE)
+            nc.vector.scalar_tensor_tensor(db[:, slots], pn[:, slots], w[:], nu[:, slots], ALU.mult, ALU.subtract)
+
         dsum = sb.tile([P, G], F32, name="dsum")
         r1 = sb.tile([P, I], F32, name="r1")
-        for g0, g1 in pieces:
-            cols = slice(g0 * PAGE, g1 * PAGE)
-            nc.vector.tensor_reduce(dsum[:, g0:g1], db[:, cols].rearrange("q (g j) -> q g j", j=PAGE), AX.X, ALU.add)
-            nc.scalar.activation(r1[:, cols].rearrange("q (g j) -> q g j", j=PAGE), dsum[:, g0:g1].unsqueeze(2).to_broadcast([P, g1 - g0, PAGE]),
-                                 ACT.Copy, scale=ntr[:])
-        for g0, g1 in pieces:
-            cols = slice(g0 * PAGE, g1 * PAGE)
-            nc.vector.tensor_tensor(gf[:].indirect(offsets[:, g0:g1]), db[:, cols], r1[:, cols], ALU.add)
+        for g0, g1 in SCATTER_PAGES:
+            slots = slice(g0 * PAGE, g1 * PAGE)
+            nc.vector.tensor_reduce(dsum[:, g0:g1], by_page(db[:, slots]), AX.X, ALU.add)
+            nc.scalar.activation(by_page(r1[:, slots]), dsum[:, g0:g1].unsqueeze(2).to_broadcast([P, g1 - g0, PAGE]),
+                                 ACT.Copy, scale=centre[:])
+        for g0, g1 in SCATTER_PAGES:
+            slots = slice(g0 * PAGE, g1 * PAGE)
+            nc.vector.tensor_tensor(gf[:].indirect(offsets[:, g0:g1]), db[:, slots], r1[:, slots], ALU.add)
 
         res = sb.tile([P, T], F32, name="res")
-        t0 = 0
+        first = 0
         for n, width in enumerate(OUT_CHUNKS):
-            cols = slice(t0, t0 + width)
+            cols = slice(first, first + width)
             nc.vector.tensor_tensor(res[:, cols], gf[:, cols], old_sb[:, cols], ALU.add)
             (nc.sync if n % 2 == 0 else nc.scalar).dma_start(out[:, cols], res[:, cols])
-            t0 += width
+            first += width

from contextlib import ExitStack

import concourse.mybir as mybir
from concourse.masks import make_identity

D, T, I, Q, G = 512, 2048, 512, 128, 32
FLOPS = 2 * 2 * D * I * Q

F32 = mybir.dt.float32
BF16 = mybir.dt.bfloat16
I32 = mybir.dt.int32
U32 = mybir.dt.uint32
U16 = mybir.dt.uint16
U8 = mybir.dt.uint8
FP8X4 = mybir.dt.float8_e4m3fn_x4
ALU = mybir.AluOpType
ACT = mybir.ActivationFunctionType
AX = mybir.AxisListType

P = 128
PACK = 4
QUADRANTS = 4
PAGE = I // G
HALF = I // 2
HALF_PAGES = G // 2
GRAD_SCALE = 512.0
KEY_FIRST_ROW = 0
VAL_FIRST_ROW = 4
SCATTER_PAGES = [(0, 8), (8, G)]
OUT_CHUNKS = [448, 448, 448, 384, 320]


def tile_attend_bpagecentred_s_kernel(tc, query, keys_words, keys_scales, trust, gout, vals_words, vals_scales, size, old, offs, out):
    nc = tc.nc
    with ExitStack() as ctx:
        sb = ctx.enter_context(tc.tile_pool(name="sb", bufs=1))
        ps = ctx.enter_context(tc.psum_pool(name="ps", bufs=1))

        offsets = sb.tile([P, I // 16], U16, name="offsets")
        nc.sync.dma_start(offsets[:], offs)

        q_raw = sb.tile([P, PACK, Q], F32, name="q_raw", tag="raw")
        nc.sync.dma_start(q_raw[:], query.rearrange("(p j) w -> p j w", j=PACK))
        trust_sb = sb.tile([P, 1], F32, name="trust_sb")
        nc.sync.dma_start(trust_sb[:], trust)

        ks = sb.tile([P, T], U8, name="ks", tag="ks_vw", align_bytes=64)
        vs = sb.tile([P, T], U8, name="vs", align_bytes=64)
        gf = sb.tile([P, T], F32, name="gf", align_bytes=64)
        nc.vector.memset(ks[:, : T // 2].bitcast(I32), 0)
        nc.gpsimd.memset(ks[:, T // 2 :].bitcast(I32), 0)
        nc.vector.memset(vs[:].bitcast(I32), 0)
        nc.vector.memset(gf[:], 0.0)

        def load_scale_rows(plane, scales, first_row):
            for z in range(QUADRANTS):
                row = 32 * z + first_row
                nc.sync.dma_start(plane[row : row + 4, :].bitcast(I32), scales[0, 4 * z : 4 * z + 4, :].bitcast(I32))

        def load_words(tile, words):
            nc.sync.dma_start(tile[:], words[0].rearrange("p n t -> p (n t)").bitcast(I32))

        load_scale_rows(ks, keys_scales, KEY_FIRST_ROW)
        kw = sb.tile([P, T], I32, name="kw", tag="kw_old", align_bytes=64)
        load_words(kw, keys_words)
        load_scale_rows(vs, vals_scales, VAL_FIRST_ROW)

        size_col = sb.tile([P, PACK], F32, name="size_col")
        nc.gpsimd.dma_start(size_col[:], size[0].rearrange("(p c) -> p c", c=PACK))
        ident = sb.tile([P, P], F32, name="ident")
        make_identity(nc, ident[:])
        centre = sb.tile([P, 1], F32, name="centre")
        nc.gpsimd.tensor_scalar(centre[:], trust_sb[:], -1.0 / PAGE, 0.0, ALU.mult, ALU.add)

        def quantise(raw, name):
            grouped = sb.tile([P, Q, PACK], BF16, name=name + "_bf", tag=name + "_bf", align_bytes=64)
            nc.scalar.copy(grouped[:], raw[:].rearrange("p j w -> p w j"))
            codes = sb.tile([P, Q], U32, name=name + "_codes", tag="codes", align_bytes=64)
            scales = sb.tile([P, Q], U8, name=name + "_scales", align_bytes=64)
            nc.vector.quantize_mx(out=codes[:].bitcast(FP8X4), scales=scales[:], in_=grouped[:].rearrange("p w j -> p (w j)"))
            return codes, scales

        def half_offsets(h):
            return offsets[:, h * (HALF // 16) : (h + 1) * (HALF // 16)]

        def product(words, gathered_scales, first_row, codes, scales, name, results, tags):
            for h in range(2):
                gathered = sb.tile([P, HALF], U32, name=name + "_wg%d" % h, tag=tags[h], align_bytes=64)
                nc.vector.tensor_copy(gathered[:], words[:].bitcast(U32).indirect(half_offsets(h)))
                nc.tensor.matmul_mx(out=results[h], lhsT=codes[:].bitcast(FP8X4), lhsT_scale=scales[:], rhs=gathered[:].bitcast(FP8X4),
                                    rhs_scale=gathered_scales[h][first_row:P, :], start=True, stop=True)

        def by_page(ap):
            return ap.rearrange("q (g j) -> q g j", j=PAGE)

        ksg = sb.tile([P, I], U8, name="ksg", align_bytes=64)
        nc.vector.tensor_copy(ksg[:], ks[:].indirect(offsets[:]))
        vw = sb.tile([P, T], I32, name="vw", tag="ks_vw", align_bytes=64)
        load_words(vw, vals_words)
        q_codes, q_scales = quantise(q_raw, "q")
        g_raw = sb.tile([P, PACK, Q], F32, name="g_raw", tag="raw")
        nc.scalar.dma_start(g_raw[:], gout.rearrange("(p j) w -> p j w", j=PACK))
        a = [ps.tile([P, HALF], F32, name="a_bank%d" % h, tag="a_bank%d" % h) for h in range(2)]
        product(kw, [ksg[:, :HALF], ksg[:, HALF:]], KEY_FIRST_ROW, q_codes, q_scales, "a", [a[0][:], a[1][:]], ["a_wg0", "wg1"])
        old_sb = sb.tile([P, T], F32, name="old_sb", tag="kw_old", align_bytes=64)
        nc.sync.dma_start(old_sb[:], old)
        vsg0 = sb.tile([P, HALF], U8, name="vsg0", align_bytes=64)
        nc.vector.tensor_copy(vsg0[:], vs[:].indirect(half_offsets(0)))

        asum = sb.tile([P, G], F32, name="asum")
        b = sb.tile([P, G, PAGE], F32, name="b")
        for h in range(2):
            nc.vector.tensor_reduce(asum[:, h * HALF_PAGES : (h + 1) * HALF_PAGES], by_page(a[h][:]), AX.X, ALU.add)
        for h in range(2):
            pages = slice(h * HALF_PAGES, (h + 1) * HALF_PAGES)
            nc.vector.scalar_tensor_tensor(b[:, pages, :], asum[:, pages].unsqueeze(2).to_broadcast([P, HALF_PAGES, PAGE]), centre[:],
                                           by_page(a[h][:]), ALU.mult, ALU.add)

        size_ps = ps.tile([P, PACK, P], F32, name="size_ps", tag="a_bank0")
        for c in range(PACK):
            nc.tensor.transpose(size_ps[:, c, :], size_col[:, c : c + 1].to_broadcast([P, P]), ident[:])

        nsize = sb.tile([P, I], F32, name="nsize")
        nc.scalar.activation(nsize[:].rearrange("q (s c) -> q s c", c=PACK), size_ps[:].rearrange("q c s -> q s c"), ACT.Copy, scale=-GRAD_SCALE)
        g_codes, g_scales = quantise(g_raw, "g")

        nmax = sb.tile([P, 1], F32, name="nmax")
        negb = sb.tile([P, I], F32, name="negb", tag="negb_vsg", align_bytes=64)
        nc.vector.tensor_scalar(negb[:], b[:].rearrange("q g j -> q (g j)"), -1.0, None, ALU.mult, ALU.min, accum_out=nmax[:])
        vsg1 = sb.tile([P, HALF], U8, name="vsg1", tag="negb_vsg", align_bytes=64)
        nc.vector.tensor_copy(vsg1[:], vs[:].indirect(half_offsets(1)))
        p = sb.tile([P, I], F32, name="p")
        z = sb.tile([P, 1], F32, name="z")
        nc.scalar.activation(p[:], b[:].rearrange("q g j -> q (g j)"), ACT.Exp, bias=nmax[:], accum_out=z[:])

        c0 = ps.tile([P, I], F32, name="c0")
        product(vw, [vsg0[:], vsg1[:]], VAL_FIRST_ROW, g_codes, g_scales, "c", [c0[:, :HALF], c0[:, HALF:]], ["g_bf", "wg1"])
        p_nsize = sb.tile([P, I], F32, name="p_nsize")
        rz = sb.tile([P, 1], F32, name="rz", tag="g_bf", align_bytes=64)
        nc.vector.reciprocal(rz[:], z[:])
        nc.gpsimd.tensor_tensor(p_nsize[:], p[:], nsize[:], ALU.mult)
        pn = sb.tile([P, I], F32, name="pn")
        nc.scalar.activation(pn[:], p[:], ACT.Copy, scale=rz[:])

        nu = sb.tile([P, I], F32, name="nu")
        w = sb.tile([P, 1], F32, name="w")
        nc.vector.scalar_tensor_tensor(nu[:], c0[:], rz[:], p_nsize[:], ALU.mult, ALU.mult, accum_out=w[:])
        db = sb.tile([P, I], F32, name="db")
        for g0, g1 in SCATTER_PAGES:
            slots = slice(g0 * PAGE, g1 * PAGE)
            nc.vector.scalar_tensor_tensor(db[:, slots], pn[:, slots], w[:], nu[:, slots], ALU.mult, ALU.subtract)

        dsum = sb.tile([P, G], F32, name="dsum")
        r1 = sb.tile([P, I], F32, name="r1")
        for g0, g1 in SCATTER_PAGES:
            slots = slice(g0 * PAGE, g1 * PAGE)
            nc.vector.tensor_reduce(dsum[:, g0:g1], by_page(db[:, slots]), AX.X, ALU.add)
            nc.scalar.activation(by_page(r1[:, slots]), dsum[:, g0:g1].unsqueeze(2).to_broadcast([P, g1 - g0, PAGE]),
                                 ACT.Copy, scale=centre[:])
        for g0, g1 in SCATTER_PAGES:
            slots = slice(g0 * PAGE, g1 * PAGE)
            nc.vector.tensor_tensor(gf[:].indirect(offsets[:, g0:g1]), db[:, slots], r1[:, slots], ALU.add)

        res = sb.tile([P, T], F32, name="res")
        first = 0
        for n, width in enumerate(OUT_CHUNKS):
            cols = slice(first, first + width)
            nc.vector.tensor_tensor(res[:, cols], gf[:, cols], old_sb[:, cols], ALU.add)
            (nc.sync if n % 2 == 0 else nc.scalar).dma_start(out[:, cols], res[:, cols])
            first += width
